import numpy as np
import ml_dtypes


def mxq(x, axis, fmt="e4m3"):
    dtype, down = {"e4m3": (ml_dtypes.float8_e4m3fn, 7), "e5m2": (ml_dtypes.float8_e5m2, 14)}[fmt]
    v = np.moveaxis(np.asarray(x, np.float32).astype(ml_dtypes.bfloat16).astype(np.float64), axis, -1)
    blocks = v.reshape(v.shape[:-1] + (-1, 32))
    amax = np.abs(blocks).max(-1, keepdims=True)
    byte = np.maximum(np.where(amax > 0, np.frexp(amax)[1] - 1 + 127, 0) - down, 1)
    scale = np.exp2(byte - 127.0)
    codes = (blocks / scale).astype(np.float32).astype(dtype).astype(np.float64)
    return np.moveaxis((codes * scale).reshape(v.shape), -1, axis)


WIDE = False


def mx_kscale(k):
    if not WIDE:
        return np.ones(k)
    levels = np.array([10, -10, 5, -5, 0])
    if k % 512:
        return np.exp2(np.random.permutation(np.resize(levels, k // 32))).repeat(32)
    a = np.empty((k // 512, 16))
    for p in range(k // 512):
        a[p, :8] = np.random.permutation(np.resize(levels, 8))
        for g in range(8):
            far = levels[np.abs(levels - a[p, g]) >= 10]
            a[p, g + 8] = far[np.random.randint(len(far))]
    return np.exp2(a.ravel()).repeat(32)


def f64(x):
    return np.asarray(x).astype(np.float64)


def striped(idx):
    return np.tile(np.asarray(idx).reshape(-1, 16).T, (8, 1)).astype(np.uint16)


def unstriped(offs):
    return offs[:16].T.reshape(-1).astype(np.int64)


E2M1 = np.array([0.0, 0.5, 1.0, 1.5, 2.0, 3.0, 4.0, 6.0, -0.0, -0.5, -1.0, -1.5, -2.0, -3.0, -4.0, -6.0])


def pack_weight(w, fmt):
    k, n = w.shape
    w = f64(np.asarray(w, np.float32).astype(ml_dtypes.bfloat16)).reshape(k // 32, 32, n)
    amax = np.abs(w).max(1)
    if fmt == "e4m3":
        byte = np.frexp(amax)[1] - 1 + 127 - 7
    else:
        mant, ex = np.frexp(amax / 6.0)
        byte = np.where(mant > 0.5, ex, ex - 1) + 127
    byte = np.clip(np.where(amax > 0, byte, 1), 1, 254)
    scaled = (w * np.exp2(127.0 - byte)[:, None, :]).reshape(k, n).astype(np.float32)
    by_word = np.ascontiguousarray(scaled.reshape(k // 512, 128, 4, n).transpose(0, 1, 3, 2))
    if fmt == "e4m3":
        words = by_word.astype(ml_dtypes.float8_e4m3fn).view(np.uint8)
    else:
        c = by_word.astype(ml_dtypes.float4_e2m1fn).view(np.uint8) & 0xF
        words = (c[..., 0::2] | (c[..., 1::2] << 4)).reshape(k // 512, 128, 2 * n)
    return np.ascontiguousarray(words), np.ascontiguousarray(byte.astype(np.uint8).reshape(k // 512, 16, n))


def unpack_weight(words, scales, fmt):
    g, _, n = scales.shape
    words = np.ascontiguousarray(words).reshape(g, 128, n, -1)
    if fmt == "e4m3":
        vals = words.view(ml_dtypes.float8_e4m3fn).astype(np.float64)
    else:
        nib = np.empty((g, 128, n, 4), np.uint8)
        nib[..., 0::2] = words & 0xF
        nib[..., 1::2] = words >> 4
        vals = E2M1[nib]
    vals = vals * np.repeat(np.exp2(scales.astype(np.float64) - 127.0), 8, axis=1)[..., None]
    return vals.transpose(0, 1, 3, 2).reshape(g * 512, n)


K, T, J, R, F, Z, X, O, N, L, E = 512, 1024, 256, 512, 512, 1024, 512, 128, 256, 512, 512


def setup_inputs():
    n = np.random.standard_normal
    idx = np.random.permutation(T)[:J]
    idx2 = np.random.permutation(Z)[:J]
    idx3 = np.random.permutation(X)[:O]
    idx4 = np.random.permutation(J)[:O]
    idx5 = np.random.permutation(J)[:O]
    idx6 = np.random.permutation(E)[:O]
    idx7 = np.random.permutation(E)[:O]
    ff = mx_kscale(F)
    fk = mx_kscale(K)
    fr = mx_kscale(R)
    fl = mx_kscale(L)
    xop = pack_weight(n((F, Z)) / ff[:, None], "e4m3")
    wp = pack_weight(n((K, R)) * 1 / np.sqrt(K) / fk[:, None] * fr, "e2m1")
    w2p = pack_weight(n((F, R)) * 1 / np.sqrt(F) * ff[:, None], "e2m1")
    wbp = pack_weight(n((R, N)) * 1 / np.sqrt(R) / fr[:, None], "e2m1")
    sxp = pack_weight(n((L, O)) / fl[:, None], "e4m3")
    wsp = pack_weight(n((L, N)) * 1 / np.sqrt(L) * fl[:, None], "e2m1")
    return {
        "xo_words": xop[0],
        "xo_scales": xop[1],
        "cq": (np.random.randint(-7, 8, (K, T)).astype(np.float64)).astype(np.float32),
        "gs": (np.random.uniform(0.1, 0.4, (K, 1)) * fk[:, None]).astype(np.float32),
        "w_words": wp[0],
        "w_scales": wp[1],
        "w2_words": w2p[0],
        "w2_scales": w2p[1],
        "tb": (n((R, X)) * 0.9).astype(np.float32),
        "wb_words": wbp[0],
        "wb_scales": wbp[1],
        "sx_words": sxp[0],
        "sx_scales": sxp[1],
        "ws_words": wsp[0],
        "ws_scales": wsp[1],
        "offs": striped(idx),
        "offs2": striped(idx2),
        "offs3": striped(idx3),
        "offs4": striped(idx4),
        "offs5": striped(idx5),
        "offs6": striped(idx6),
        "offs7": striped(idx7),
    }


def reference(xo_words, xo_scales, cq, gs, w_words, w_scales, w2_words, w2_scales, tb, wb_words, wb_scales, sx_words, sx_scales, ws_words, ws_scales, offs, offs2, offs3, offs4, offs5, offs6, offs7):
    idx = unstriped(offs)
    idx2 = unstriped(offs2)
    idx3 = unstriped(offs3)
    idx4 = unstriped(offs4)
    idx5 = unstriped(offs5)
    idx6 = unstriped(offs6)
    idx7 = unstriped(offs7)
    xou = unpack_weight(xo_words, xo_scales, "e4m3")
    wu = unpack_weight(w_words, w_scales, "e2m1")
    w2u = unpack_weight(w2_words, w2_scales, "e2m1")
    wbu = unpack_weight(wb_words, wb_scales, "e2m1")
    sxu = unpack_weight(sx_words, sx_scales, "e4m3")
    wsu = unpack_weight(ws_words, ws_scales, "e2m1")
    x1 = f64(cq)[:, idx] * f64(gs)
    x1q = mxq(x1, 0, "e4m3")
    a = wu.T @ x1q
    xoidx2g = xou[:, idx2]
    b = w2u.T @ xoidx2g
    la = a[:, 0:1]
    lb = b[:, 0:1]
    la2 = a[:, 128:129]
    hid = np.maximum(f64(tb)[:, idx3] * la, a[:, idx4] * lb) - b[:, idx5] * la2
    hidq = mxq(hid, 0, "e4m3")
    p = wbu.T @ hidq + wsu.T @ sxu
    pa = np.zeros((N, E))
    pa[:, idx6] = p
    pb = np.zeros((N, E))
    pb[:, idx7] = p
    y = pa + pb
    return y

@@ -1,0 +1,222 @@
+from contextlib import ExitStack
+
+import concourse.mybir as mybir
+
+F32 = mybir.dt.float32
+BF16 = mybir.dt.bfloat16
+I32 = mybir.dt.int32
+U32 = mybir.dt.uint32
+U16 = mybir.dt.uint16
+U8 = mybir.dt.uint8
+FP8X4 = mybir.dt.float8_e4m3fn_x4
+FP4X4 = mybir.dt.float4_e2m1fn_x4
+COPY = mybir.ActivationFunctionType.Copy
+ALU = mybir.AluOpType
+
+P = 128
+PACK = 4
+QUAD = 32
+T, J, R, Z, X, O, N, E = 1024, 256, 512, 1024, 512, 128, 256, 512
+
+FLOPS = 335544320
+
+
+def tile_list_leadlevel_codednote_further_pagetwice_kernel(
+    tc, xo_words, xo_scales, cq, gs, w_words, w_scales, w2_words, w2_scales, tb, wb_words, wb_scales,
+    sx_words, sx_scales, ws_words, ws_scales, offs, offs2, offs3, offs4, offs5, offs6, offs7, out
+):
+    nc = tc.nc
+
+    def by_quadrant(scales):
+        return scales[0].bitcast(I32).rearrange("(q r) n -> r q n", r=PACK)
+
+    with ExitStack() as ctx:
+        lists = ctx.enter_context(tc.tile_pool(name="lists", bufs=1))
+        sb = ctx.enter_context(tc.tile_pool(name="sb", bufs=1))
+        psum = ctx.enter_context(tc.psum_pool(name="psum", bufs=1))
+
+        def load_list(src, name):
+            tile = lists.tile([P, src.shape[1]], U16, name=name)
+            nc.sync.dma_start(tile[:], src)
+            return tile
+
+        def load_bytes(src, width, name):
+            tile = sb.tile([P, width], U8, name=name, align_bytes=64)
+            nc.sync.dma_start(tile[:].bitcast(I32), src.bitcast(I32))
+            return tile
+
+        cq_rows = cq.rearrange("(p i) t -> i p t", i=PACK)
+        tb_rows = tb.rearrange("(p i) x -> i p x", i=PACK)
+        cq_t = [sb.tile([P, T], F32, name=f"cq{i}") for i in range(PACK)]
+        tb_t = [sb.tile([P, X], F32, name=f"tb{i}") for i in range(PACK)]
+
+        nc.sync.dma_start(cq_t[0][:], cq_rows[0])
+        idx = load_list(offs, "idx")
+        for i in range(1, PACK):
+            nc.sync.dma_start(cq_t[i][:], cq_rows[i])
+        w_raw = load_bytes(w_words[0], 2 * R, "w_raw")
+        idx2 = load_list(offs2, "idx2")
+        w2_raw = load_bytes(w2_words[0], 2 * R, "w2_raw")
+        xo_t = sb.tile([P, Z], I32, name="xo_t")
+        nc.sync.dma_start(xo_t[:], xo_words[0].rearrange("p c r -> p (c r)").bitcast(I32))
+        idx3 = load_list(offs3, "idx3")
+        nc.sync.dma_start(tb_t[0][:], tb_rows[0])
+        idx4 = load_list(offs4, "idx4")
+        idx5 = load_list(offs5, "idx5")
+        for i in range(1, PACK):
+            nc.sync.dma_start(tb_t[i][:], tb_rows[i])
+        ws_t = load_bytes(ws_words[0], 2 * N, "ws_t")
+        sx_t = load_bytes(sx_words[0].rearrange("p c r -> p (c r)"), 4 * O, "sx_t")
+        wb_t = load_bytes(wb_words[0], 2 * N, "wb_t")
+        idx6 = load_list(offs6, "idx6")
+        idx7 = load_list(offs7, "idx7")
+
+        gs_t = sb.tile([P, PACK], F32, name="gs_t")
+        nc.scalar.dma_start(gs_t[:], gs.rearrange("(p i) o -> p (i o)", i=PACK))
+        late_stage = sb.tile([PACK, 4, (N + N + O) // 4], I32, name="late_stage")
+        nc.scalar.dma_start(late_stage[:, :, 0 : N // 4], by_quadrant(wb_scales))
+        nc.scalar.dma_start(late_stage[:, :, N // 4 : 2 * N // 4], by_quadrant(ws_scales))
+        nc.scalar.dma_start(late_stage[:, :, 2 * N // 4 :], by_quadrant(sx_scales))
+
+        w_stage = sb.tile([PACK, 4, 2 * R // 4], I32, name="w_stage")
+        nc.gpsimd.dma_start(w_stage[:, :, 0 : R // 4], by_quadrant(w_scales))
+        nc.gpsimd.dma_start(w_stage[:, :, R // 4 :], by_quadrant(w2_scales))
+        xo_stage = sb.tile([P, 4, Z // 4], I32, name="xo_stage")
+        nc.vector.memset(xo_stage[64:96, :, :], 0)
+        nc.gpsimd.dma_start(xo_stage[64 : 64 + PACK, :, :], by_quadrant(xo_scales))
+
+        w_plane_raw = sb.tile([P, 2 * R], U8, name="w_plane_raw")
+        late_plane = sb.tile([P, N + N + O], U8, name="late_plane", align_bytes=64)
+        nc.vector.memset(w_plane_raw[:].bitcast(I32), 0)
+        nc.vector.memset(late_plane[:].bitcast(I32), 0)
+        pages = [[sb.tile([P, E], F32, name=f"page{h}{s}") for s in range(2)] for h in range(2)]
+        for h in range(2):
+            for s in range(2):
+                nc.vector.memset(pages[h][s][:], 0.0)
+
+        for q in range(4):
+            nc.vector.tensor_copy(late_plane[QUAD * q : QUAD * q + PACK, :].bitcast(I32), late_stage[:, q, :])
+        for q in range(4):
+            nc.vector.tensor_copy(w_plane_raw[QUAD * q : QUAD * q + PACK, :].bitcast(I32), w_stage[:, q, :])
+        w_plane = sb.tile([P, 2 * R], U8, name="w_plane", align_bytes=64)
+        nc.vector.tensor_copy(
+            w_plane[:].rearrange("p (u t m) -> p u t m", u=2, t=PACK),
+            w_plane_raw[:].rearrange("p (u m t) -> p u t m", u=2, t=PACK),
+        )
+        xo_plane = sb.tile([P, Z], U8, name="xo_plane")
+        for q in range(4):
+            nc.vector.tensor_copy(xo_plane[QUAD * q : QUAD * (q + 1), :].bitcast(I32), xo_stage[64:96, q, :])
+        note_scales = sb.tile([P, J], U8, name="note_scales", align_bytes=64)
+        nc.vector.tensor_copy(note_scales[:], xo_plane[:].indirect(idx2[:]))
+
+        x1 = sb.tile([P, PACK, J], BF16, name="x1")
+        x1_il = sb.tile([P, J, PACK], BF16, name="x1_il", align_bytes=64)
+        for i in range(PACK):
+            nc.scalar.activation(x1[:, i, :], cq_t[i][:].indirect(idx[:]), COPY, scale=gs_t[:, i : i + 1])
+            if i % 2 == 1:
+                nc.vector.tensor_copy(x1_il[:, :, i - 1 : i + 1], x1[:, i - 1 : i + 1, :].rearrange("p t j -> p j t"))
+        x1_codes = sb.tile([P, J], U32, name="x1_codes", align_bytes=64)
+        x1_scales = sb.tile([P, J], U8, name="x1_scales", align_bytes=64)
+
+        w_t = sb.tile([P, 2 * R], U8, name="w_t", align_bytes=64)
+        w2_t = sb.tile([P, 2 * R], U8, name="w2_t", align_bytes=64)
+        nc.vector.tensor_copy(
+            w_t[:].bitcast(U16).rearrange("p (t m) -> p t m", t=PACK),
+            w_raw[:].bitcast(U16).rearrange("p (m t) -> p t m", t=PACK),
+        )
+        nc.scalar.copy(
+            w2_t[:].bitcast(U16).rearrange("p (t m) -> p t m", t=PACK),
+            w2_raw[:].bitcast(U16).rearrange("p (m t) -> p t m", t=PACK),
+        )
+        nc.vector.quantize_mx(
+            out=x1_codes[:].bitcast(FP8X4), scales=x1_scales[:], in_=x1_il[:].rearrange("p j t -> p (j t)")
+        )
+        note_words = sb.tile([P, J], U32, name="note_words", align_bytes=64)
+        nc.vector.tensor_copy(note_words[:], xo_t[:].bitcast(U32).indirect(idx2[:]))
+
+        a_ps = [psum.tile([P, J], F32, name=f"a_ps{t}") for t in range(PACK)]
+        b_ps = [psum.tile([P, 2, J], F32, name=f"b_ps{u}") for u in range(2)]
+        for t in range(PACK):
+            nc.tensor.matmul_mx(
+                out=a_ps[t][:],
+                lhsT=w_t[:, 2 * P * t : 2 * P * (t + 1)].bitcast(FP4X4),
+                lhsT_scale=w_plane[:, P * t : P * (t + 1)],
+                rhs=x1_codes[:].bitcast(FP8X4),
+                rhs_scale=x1_scales[:],
+                start=True,
+                stop=True,
+            )
+        for t in range(PACK):
+            nc.tensor.matmul_mx(
+                out=b_ps[t // 2][:, t % 2, :],
+                lhsT=w2_t[:, 2 * P * t : 2 * P * (t + 1)].bitcast(FP4X4),
+                lhsT_scale=w_plane[:, R + P * t : R + P * (t + 1)],
+                rhs=note_words[:].bitcast(FP8X4),
+                rhs_scale=note_scales[:],
+                start=True,
+                stop=True,
+            )
+        p_ps = [psum.tile([P, O], F32, name=f"p_ps{h}") for h in range(2)]
+        for h in range(2):
+            nc.tensor.matmul_mx(
+                out=p_ps[h][:],
+                lhsT=ws_t[:, 2 * P * h : 2 * P * (h + 1)].bitcast(FP4X4),
+                lhsT_scale=late_plane[:, N + P * h : N + P * (h + 1)],
+                rhs=sx_t[:].bitcast(FP8X4),
+                rhs_scale=late_plane[:, 2 * N :],
+                start=True,
+                stop=False,
+            )
+
+        a_t = [sb.tile([P, J], F32, name=f"a{t}") for t in range(PACK)]
+        b_t = [sb.tile([P, J], F32, name=f"b{t}") for t in range(PACK)]
+        level = sb.tile([P, PACK, O], F32, name="level")
+        lead = sb.tile([P, PACK, O], F32, name="lead")
+        minus = sb.tile([P, PACK, O], F32, name="minus")
+        larger = sb.tile([P, PACK, O], F32, name="larger")
+        hid = sb.tile([P, O, PACK], BF16, name="hid", align_bytes=64)
+        nc.scalar.copy(a_t[0][:], a_ps[0][:])
+        for t in range(PACK):
+            if t + 1 < PACK:
+                nc.vector.tensor_copy(a_t[t + 1][:], a_ps[t + 1][:])
+            nc.vector.tensor_copy(b_t[t][:], b_ps[t // 2][:, t % 2, :])
+        nc.scalar.activation(level[:, 0, :], tb_t[0][:].indirect(idx3[:]), COPY, scale=a_t[0][:, 0:1])
+        for t in range(PACK):
+            if t + 1 < PACK:
+                nc.scalar.activation(
+                    level[:, t + 1, :], tb_t[t + 1][:].indirect(idx3[:]), COPY, scale=a_t[t + 1][:, 0:1]
+                )
+            nc.scalar.activation(lead[:, t, :], a_t[t][:].indirect(idx4[:]), COPY, scale=b_t[t][:, 0:1])
+            nc.scalar.activation(minus[:, t, :], b_t[t][:].indirect(idx5[:]), COPY, scale=a_t[t][:, P : P + 1])
+            nc.vector.tensor_tensor(larger[:, t, :], level[:, t, :], lead[:, t, :], ALU.max)
+            nc.vector.tensor_tensor(hid[:, :, t], larger[:, t, :], minus[:, t, :], ALU.subtract)
+
+        hid_codes = sb.tile([P, O], U32, name="hid_codes", align_bytes=64)
+        hid_scales = sb.tile([P, O], U8, name="hid_scales", align_bytes=64)
+        nc.vector.quantize_mx(
+            out=hid_codes[:].bitcast(FP8X4), scales=hid_scales[:], in_=hid[:].rearrange("p o t -> p (o t)")
+        )
+        for h in range(2):
+            nc.tensor.matmul_mx(
+                out=p_ps[h][:],
+                lhsT=wb_t[:, 2 * P * h : 2 * P * (h + 1)].bitcast(FP4X4),
+                lhsT_scale=late_plane[:, P * h : P * (h + 1)],
+                rhs=hid_codes[:].bitcast(FP8X4),
+                rhs_scale=hid_scales[:],
+                start=False,
+                stop=True,
+            )
+
+        p_t = [sb.tile([P, O], F32, name=f"p{h}") for h in range(2)]
+        nc.vector.tensor_copy(p_t[0][:], p_ps[0][:])
+        nc.scalar.copy(p_t[1][:], p_ps[1][:])
+        nc.vector.tensor_copy(pages[0][0][:].indirect(idx6[:]), p_t[0][:])
+        nc.scalar.activation(pages[0][1][:].indirect(idx7[:]), p_t[0][:], COPY)
+        nc.vector.tensor_copy(pages[1][1][:].indirect(idx7[:]), p_t[1][:])
+        nc.scalar.activation(pages[1][0][:].indirect(idx6[:]), p_t[1][:], COPY)
+        for h in range(2):
+            for c in range(2):
+                cols = slice(c * E // 2, (c + 1) * E // 2)
+                y = sb.tile([P, E // 2], F32, name=f"y{h}{c}")
+                nc.vector.tensor_tensor(y[:], pages[h][0][:, cols], pages[h][1][:, cols], ALU.add)
+                nc.sync.dma_start(out[P * h : P * (h + 1), cols], y[:])

@@ -33,6 +33,7 @@ def tile_list_leadlevel_codednote_further_pagetwice_kernel(
     with ExitStack() as ctx:
         lists = ctx.enter_context(tc.tile_pool(name="lists", bufs=1))
         sb = ctx.enter_context(tc.tile_pool(name="sb", bufs=1))
+        reused = ctx.enter_context(tc.tile_pool(name="reused", bufs=1))
         psum = ctx.enter_context(tc.psum_pool(name="psum", bufs=1))
 
         def load_list(src, name):
@@ -50,14 +51,14 @@ def tile_list_leadlevel_codednote_further_pagetwice_kernel(
         cq_t = [sb.tile([P, T], F32, name=f"cq{i}") for i in range(PACK)]
         tb_t = [sb.tile([P, X], F32, name=f"tb{i}") for i in range(PACK)]
 
-        nc.sync.dma_start(cq_t[0][:], cq_rows[0])
         idx = load_list(offs, "idx")
+        nc.sync.dma_start(cq_t[0][:], cq_rows[0])
+        idx2 = load_list(offs2, "idx2")
         for i in range(1, PACK):
             nc.sync.dma_start(cq_t[i][:], cq_rows[i])
         w_raw = load_bytes(w_words[0], 2 * R, "w_raw")
-        idx2 = load_list(offs2, "idx2")
         w2_raw = load_bytes(w2_words[0], 2 * R, "w2_raw")
-        xo_t = sb.tile([P, Z], I32, name="xo_t")
+        xo_t = reused.tile([P, Z], I32, name="xo_t", offset=0)
         nc.sync.dma_start(xo_t[:], xo_words[0].rearrange("p c r -> p (c r)").bitcast(I32))
         idx3 = load_list(offs3, "idx3")
         nc.sync.dma_start(tb_t[0][:], tb_rows[0])
@@ -65,6 +66,10 @@ def tile_list_leadlevel_codednote_further_pagetwice_kernel(
         idx5 = load_list(offs5, "idx5")
         for i in range(1, PACK):
             nc.sync.dma_start(tb_t[i][:], tb_rows[i])
+        late_stage = sb.tile([PACK, 4, (N + N + O) // 4], I32, name="late_stage")
+        nc.sync.dma_start(late_stage[:, :, 0 : N // 4], by_quadrant(wb_scales))
+        nc.sync.dma_start(late_stage[:, :, N // 4 : 2 * N // 4], by_quadrant(ws_scales))
+        nc.sync.dma_start(late_stage[:, :, 2 * N // 4 :], by_quadrant(sx_scales))
         ws_t = load_bytes(ws_words[0], 2 * N, "ws_t")
         sx_t = load_bytes(sx_words[0].rearrange("p c r -> p (c r)"), 4 * O, "sx_t")
         wb_t = load_bytes(wb_words[0], 2 * N, "wb_t")
@@ -73,21 +78,17 @@ def tile_list_leadlevel_codednote_further_pagetwice_kernel(
 
         gs_t = sb.tile([P, PACK], F32, name="gs_t")
         nc.scalar.dma_start(gs_t[:], gs.rearrange("(p i) o -> p (i o)", i=PACK))
-        late_stage = sb.tile([PACK, 4, (N + N + O) // 4], I32, name="late_stage")
-        nc.scalar.dma_start(late_stage[:, :, 0 : N // 4], by_quadrant(wb_scales))
-        nc.scalar.dma_start(late_stage[:, :, N // 4 : 2 * N // 4], by_quadrant(ws_scales))
-        nc.scalar.dma_start(late_stage[:, :, 2 * N // 4 :], by_quadrant(sx_scales))
-
         w_stage = sb.tile([PACK, 4, 2 * R // 4], I32, name="w_stage")
-        nc.gpsimd.dma_start(w_stage[:, :, 0 : R // 4], by_quadrant(w_scales))
-        nc.gpsimd.dma_start(w_stage[:, :, R // 4 :], by_quadrant(w2_scales))
+        nc.scalar.dma_start(w_stage[:, :, 0 : R // 4], by_quadrant(w_scales))
+        nc.scalar.dma_start(w_stage[:, :, R // 4 :], by_quadrant(w2_scales))
         xo_stage = sb.tile([P, 4, Z // 4], I32, name="xo_stage")
         nc.vector.memset(xo_stage[64:96, :, :], 0)
-        nc.gpsimd.dma_start(xo_stage[64 : 64 + PACK, :, :], by_quadrant(xo_scales))
+        nc.scalar.dma_start(xo_stage[64 : 64 + PACK, :, :], by_quadrant(xo_scales))
 
         w_plane_raw = sb.tile([P, 2 * R], U8, name="w_plane_raw")
         late_plane = sb.tile([P, N + N + O], U8, name="late_plane", align_bytes=64)
         nc.vector.memset(w_plane_raw[:].bitcast(I32), 0)
+        xo_plane = sb.tile([P, Z], U8, name="xo_plane")
         nc.vector.memset(late_plane[:].bitcast(I32), 0)
         pages = [[sb.tile([P, E], F32, name=f"page{h}{s}") for s in range(2)] for h in range(2)]
         for h in range(2):
@@ -95,19 +96,17 @@ def tile_list_leadlevel_codednote_further_pagetwice_kernel(
                 nc.vector.memset(pages[h][s][:], 0.0)
 
         for q in range(4):
-            nc.vector.tensor_copy(late_plane[QUAD * q : QUAD * q + PACK, :].bitcast(I32), late_stage[:, q, :])
-        for q in range(4):
             nc.vector.tensor_copy(w_plane_raw[QUAD * q : QUAD * q + PACK, :].bitcast(I32), w_stage[:, q, :])
         w_plane = sb.tile([P, 2 * R], U8, name="w_plane", align_bytes=64)
         nc.vector.tensor_copy(
             w_plane[:].rearrange("p (u t m) -> p u t m", u=2, t=PACK),
             w_plane_raw[:].rearrange("p (u m t) -> p u t m", u=2, t=PACK),
         )
-        xo_plane = sb.tile([P, Z], U8, name="xo_plane")
         for q in range(4):
             nc.vector.tensor_copy(xo_plane[QUAD * q : QUAD * (q + 1), :].bitcast(I32), xo_stage[64:96, q, :])
         note_scales = sb.tile([P, J], U8, name="note_scales", align_bytes=64)
         nc.vector.tensor_copy(note_scales[:], xo_plane[:].indirect(idx2[:]))
+
 
         x1 = sb.tile([P, PACK, J], BF16, name="x1")
         x1_il = sb.tile([P, J, PACK], BF16, name="x1_il", align_bytes=64)
@@ -134,11 +133,11 @@ def tile_list_leadlevel_codednote_further_pagetwice_kernel(
         note_words = sb.tile([P, J], U32, name="note_words", align_bytes=64)
         nc.vector.tensor_copy(note_words[:], xo_t[:].bitcast(U32).indirect(idx2[:]))
 
-        a_ps = [psum.tile([P, J], F32, name=f"a_ps{t}") for t in range(PACK)]
-        b_ps = [psum.tile([P, 2, J], F32, name=f"b_ps{u}") for u in range(2)]
+        a_ps = [psum.tile([P, J], F32, name=f"a_ps{t}")[:] for t in range(PACK)]
+        b_ps = [psum.tile([P, J], F32, name=f"b_ps{t}")[:] for t in range(PACK)]
         for t in range(PACK):
             nc.tensor.matmul_mx(
-                out=a_ps[t][:],
+                out=a_ps[t],
                 lhsT=w_t[:, 2 * P * t : 2 * P * (t + 1)].bitcast(FP4X4),
                 lhsT_scale=w_plane[:, P * t : P * (t + 1)],
                 rhs=x1_codes[:].bitcast(FP8X4),
@@ -148,7 +147,7 @@ def tile_list_leadlevel_codednote_further_pagetwice_kernel(
             )
         for t in range(PACK):
             nc.tensor.matmul_mx(
-                out=b_ps[t // 2][:, t % 2, :],
+                out=b_ps[t],
                 lhsT=w2_t[:, 2 * P * t : 2 * P * (t + 1)].bitcast(FP4X4),
                 lhsT_scale=w_plane[:, R + P * t : R + P * (t + 1)],
                 rhs=note_words[:].bitcast(FP8X4),
@@ -156,7 +155,24 @@ def tile_list_leadlevel_codednote_further_pagetwice_kernel(
                 start=True,
                 stop=True,
             )
-        p_ps = [psum.tile([P, O], F32, name=f"p_ps{h}") for h in range(2)]
+
+        a_t = [sb.tile([P, J], F32, name="a0")]
+        a_t.extend(reused.tile([P, J], F32, name=f"a{t}", offset=4 * J * t) for t in range(1, PACK))
+        b_t = [sb.tile([P, J], F32, name=f"b{t}") for t in range(PACK)]
+        level = sb.tile([P, PACK, O], F32, name="level")
+        lead = sb.tile([P, PACK, O], F32, name="lead")
+        hid = sb.tile([P, O, PACK], BF16, name="hid", align_bytes=64)
+        nc.scalar.copy(a_t[0][:], a_ps[0])
+        nc.vector.tensor_copy(a_t[1][:], a_ps[1])
+        for t in range(2):
+            nc.vector.tensor_copy(b_t[t][:], b_ps[t])
+        for t in range(2, PACK):
+            nc.vector.tensor_copy(a_t[t][:], a_ps[t])
+        for t in range(2, PACK):
+            nc.vector.tensor_copy(b_t[t][:], b_ps[t])
+        for q in range(4):
+            nc.vector.tensor_copy(late_plane[QUAD * q : QUAD * q + PACK, :].bitcast(I32), late_stage[:, q, :])
+        p_ps = [psum.tile([P, O], F32, name=f"p_ps{h}", tag=f"b_ps{2 + h}") for h in range(2)]
         for h in range(2):
             nc.tensor.matmul_mx(
                 out=p_ps[h][:],
@@ -168,28 +184,22 @@ def tile_list_leadlevel_codednote_further_pagetwice_kernel(
                 stop=False,
             )
 
-        a_t = [sb.tile([P, J], F32, name=f"a{t}") for t in range(PACK)]
-        b_t = [sb.tile([P, J], F32, name=f"b{t}") for t in range(PACK)]
-        level = sb.tile([P, PACK, O], F32, name="level")
-        lead = sb.tile([P, PACK, O], F32, name="lead")
-        minus = sb.tile([P, PACK, O], F32, name="minus")
-        larger = sb.tile([P, PACK, O], F32, name="larger")
-        hid = sb.tile([P, O, PACK], BF16, name="hid", align_bytes=64)
-        nc.scalar.copy(a_t[0][:], a_ps[0][:])
-        for t in range(PACK):
-            if t + 1 < PACK:
-                nc.vector.tensor_copy(a_t[t + 1][:], a_ps[t + 1][:])
-            nc.vector.tensor_copy(b_t[t][:], b_ps[t // 2][:, t % 2, :])
-        nc.scalar.activation(level[:, 0, :], tb_t[0][:].indirect(idx3[:]), COPY, scale=a_t[0][:, 0:1])
-        for t in range(PACK):
-            if t + 1 < PACK:
-                nc.scalar.activation(
-                    level[:, t + 1, :], tb_t[t + 1][:].indirect(idx3[:]), COPY, scale=a_t[t + 1][:, 0:1]
-                )
-            nc.scalar.activation(lead[:, t, :], a_t[t][:].indirect(idx4[:]), COPY, scale=b_t[t][:, 0:1])
-            nc.scalar.activation(minus[:, t, :], b_t[t][:].indirect(idx5[:]), COPY, scale=a_t[t][:, P : P + 1])
-            nc.vector.tensor_tensor(larger[:, t, :], level[:, t, :], lead[:, t, :], ALU.max)
-            nc.vector.tensor_tensor(hid[:, :, t], larger[:, t, :], minus[:, t, :], ALU.subtract)
+        for pair in (slice(0, 2), slice(2, 4)):
+            for t in range(pair.start, pair.stop):
+                nc.scalar.activation(level[:, t, :], tb_t[t][:].indirect(idx3[:]), COPY, scale=a_t[t][:, 0:1])
+            for t in range(pair.start, pair.stop):
+                nc.scalar.activation(lead[:, t, :], a_t[t][:].indirect(idx4[:]), COPY, scale=b_t[t][:, 0:1])
+            minus = sb.tile([P, 2, O], F32, name=f"minus{pair.start}", tag=f"tb{pair.stop - 1}")
+            for t in range(pair.start, pair.stop):
+                nc.scalar.activation(minus[:, t % 2, :], b_t[t][:].indirect(idx5[:]), COPY, scale=a_t[t][:, P : P + 1])
+            larger = sb.tile([P, 2, O], F32, name=f"larger{pair.start}", tag="late_stage" if pair.start else "larger")
+            nc.vector.tensor_tensor(larger[:], level[:, pair, :], lead[:, pair, :], ALU.max)
+            nc.vector.tensor_tensor(
+                hid[:, :, pair],
+                larger[:].rearrange("p t o -> p o t"),
+                minus[:].rearrange("p t o -> p o t"),
+                ALU.subtract,
+            )
 
         hid_codes = sb.tile([P, O], U32, name="hid_codes", align_bytes=64)
         hid_scales = sb.tile([P, O], U8, name="hid_scales", align_bytes=64)

@@ -81,14 +81,14 @@ def tile_list_leadlevel_codednote_further_pagetwice_kernel(
         w_stage = sb.tile([PACK, 4, 2 * R // 4], I32, name="w_stage")
         nc.scalar.dma_start(w_stage[:, :, 0 : R // 4], by_quadrant(w_scales))
         nc.scalar.dma_start(w_stage[:, :, R // 4 :], by_quadrant(w2_scales))
-        xo_stage = sb.tile([P, 4, Z // 4], I32, name="xo_stage")
-        nc.vector.memset(xo_stage[64:96, :, :], 0)
-        nc.scalar.dma_start(xo_stage[64 : 64 + PACK, :, :], by_quadrant(xo_scales))
+        xo_stage = sb.tile([PACK, 4, Z // 4], I32, name="xo_stage")
+        nc.scalar.dma_start(xo_stage[:], by_quadrant(xo_scales))
 
         w_plane_raw = sb.tile([P, 2 * R], U8, name="w_plane_raw")
         late_plane = sb.tile([P, N + N + O], U8, name="late_plane", align_bytes=64)
         nc.vector.memset(w_plane_raw[:].bitcast(I32), 0)
         xo_plane = sb.tile([P, Z], U8, name="xo_plane")
+        nc.vector.memset(xo_plane[:].bitcast(I32), 0)
         nc.vector.memset(late_plane[:].bitcast(I32), 0)
         pages = [[sb.tile([P, E], F32, name=f"page{h}{s}") for s in range(2)] for h in range(2)]
         for h in range(2):
@@ -97,13 +97,12 @@ def tile_list_leadlevel_codednote_further_pagetwice_kernel(
 
         for q in range(4):
             nc.vector.tensor_copy(w_plane_raw[QUAD * q : QUAD * q + PACK, :].bitcast(I32), w_stage[:, q, :])
+            nc.vector.tensor_copy(xo_plane[QUAD * q : QUAD * q + PACK, :].bitcast(I32), xo_stage[:, q, :])
         w_plane = sb.tile([P, 2 * R], U8, name="w_plane", align_bytes=64)
         nc.vector.tensor_copy(
             w_plane[:].rearrange("p (u t m) -> p u t m", u=2, t=PACK),
             w_plane_raw[:].rearrange("p (u m t) -> p u t m", u=2, t=PACK),
         )
-        for q in range(4):
-            nc.vector.tensor_copy(xo_plane[QUAD * q : QUAD * (q + 1), :].bitcast(I32), xo_stage[64:96, q, :])
         note_scales = sb.tile([P, J], U8, name="note_scales", align_bytes=64)
         nc.vector.tensor_copy(note_scales[:], xo_plane[:].indirect(idx2[:]))
 
@@ -112,14 +111,17 @@ def tile_list_leadlevel_codednote_further_pagetwice_kernel(
         x1_il = sb.tile([P, J, PACK], BF16, name="x1_il", align_bytes=64)
         for i in range(PACK):
             nc.scalar.activation(x1[:, i, :], cq_t[i][:].indirect(idx[:]), COPY, scale=gs_t[:, i : i + 1])
-            if i % 2 == 1:
-                nc.vector.tensor_copy(x1_il[:, :, i - 1 : i + 1], x1[:, i - 1 : i + 1, :].rearrange("p t j -> p j t"))
+            if i == 1:
+                nc.vector.tensor_copy(x1_il[:, :, 0:2], x1[:, 0:2, :].rearrange("p t j -> p j t"))
+        halves = (slice(0, J // 2), slice(J // 2, J))
+        for half in halves:
+            nc.vector.tensor_copy(x1_il[:, half, 2:4], x1[:, 2:4, half].rearrange("p t j -> p j t"))
         x1_codes = sb.tile([P, J], U32, name="x1_codes", align_bytes=64)
         x1_scales = sb.tile([P, J], U8, name="x1_scales", align_bytes=64)
 
         w_t = sb.tile([P, 2 * R], U8, name="w_t", align_bytes=64)
         w2_t = sb.tile([P, 2 * R], U8, name="w2_t", align_bytes=64)
-        nc.vector.tensor_copy(
+        nc.scalar.copy(
             w_t[:].bitcast(U16).rearrange("p (t m) -> p t m", t=PACK),
             w_raw[:].bitcast(U16).rearrange("p (m t) -> p t m", t=PACK),
         )
@@ -127,24 +129,36 @@ def tile_list_leadlevel_codednote_further_pagetwice_kernel(
             w2_t[:].bitcast(U16).rearrange("p (t m) -> p t m", t=PACK),
             w2_raw[:].bitcast(U16).rearrange("p (m t) -> p t m", t=PACK),
         )
-        nc.vector.quantize_mx(
-            out=x1_codes[:].bitcast(FP8X4), scales=x1_scales[:], in_=x1_il[:].rearrange("p j t -> p (j t)")
-        )
+        for half in halves:
+            nc.vector.quantize_mx(
+                out=x1_codes[:, half].bitcast(FP8X4),
+                scales=x1_scales[:, half],
+                in_=x1_il[:, half, :].rearrange("p j t -> p (j t)"),
+            )
         note_words = sb.tile([P, J], U32, name="note_words", align_bytes=64)
         nc.vector.tensor_copy(note_words[:], xo_t[:].bitcast(U32).indirect(idx2[:]))
 
         a_ps = [psum.tile([P, J], F32, name=f"a_ps{t}")[:] for t in range(PACK)]
         b_ps = [psum.tile([P, J], F32, name=f"b_ps{t}")[:] for t in range(PACK)]
-        for t in range(PACK):
+        a_t = [sb.tile([P, J], F32, name="a0")]
+        a_t.extend(reused.tile([P, J], F32, name=f"a{t}", offset=4 * J * t) for t in range(1, PACK))
+
+        def first_product(t, cols):
             nc.tensor.matmul_mx(
-                out=a_ps[t],
+                out=a_ps[t][:, cols],
                 lhsT=w_t[:, 2 * P * t : 2 * P * (t + 1)].bitcast(FP4X4),
                 lhsT_scale=w_plane[:, P * t : P * (t + 1)],
-                rhs=x1_codes[:].bitcast(FP8X4),
-                rhs_scale=x1_scales[:],
+                rhs=x1_codes[:, cols].bitcast(FP8X4),
+                rhs_scale=x1_scales[:, cols],
                 start=True,
                 stop=True,
             )
+
+        first_product(0, halves[0])
+        nc.scalar.copy(a_t[0][:, halves[0]], a_ps[0][:, halves[0]])
+        for t in range(1, PACK):
+            first_product(t, slice(0, J))
+        first_product(0, halves[1])
         for t in range(PACK):
             nc.tensor.matmul_mx(
                 out=b_ps[t],
@@ -156,14 +170,12 @@ def tile_list_leadlevel_codednote_further_pagetwice_kernel(
                 stop=True,
             )
 
-        a_t = [sb.tile([P, J], F32, name="a0")]
-        a_t.extend(reused.tile([P, J], F32, name=f"a{t}", offset=4 * J * t) for t in range(1, PACK))
         b_t = [sb.tile([P, J], F32, name=f"b{t}") for t in range(PACK)]
         level = sb.tile([P, PACK, O], F32, name="level")
         lead = sb.tile([P, PACK, O], F32, name="lead")
         hid = sb.tile([P, O, PACK], BF16, name="hid", align_bytes=64)
-        nc.scalar.copy(a_t[0][:], a_ps[0])
         nc.vector.tensor_copy(a_t[1][:], a_ps[1])
+        nc.scalar.copy(a_t[0][:, halves[1]], a_ps[0][:, halves[1]])
         for t in range(2):
             nc.vector.tensor_copy(b_t[t][:], b_ps[t])
         for t in range(2, PACK):

@@ -66,10 +66,12 @@ def tile_list_leadlevel_codednote_further_pagetwice_kernel(
         idx5 = load_list(offs5, "idx5")
         for i in range(1, PACK):
             nc.sync.dma_start(tb_t[i][:], tb_rows[i])
-        late_stage = sb.tile([PACK, 4, (N + N + O) // 4], I32, name="late_stage")
-        nc.sync.dma_start(late_stage[:, :, 0 : N // 4], by_quadrant(wb_scales))
-        nc.sync.dma_start(late_stage[:, :, N // 4 : 2 * N // 4], by_quadrant(ws_scales))
-        nc.sync.dma_start(late_stage[:, :, 2 * N // 4 :], by_quadrant(sx_scales))
+        late_stage = sb.tile([2 * QUAD, 2, (N + N + O) // 4], I32, name="late_stage")
+        nc.vector.memset(late_stage[:], 0)
+        for scales, first, width in ((wb_scales, 0, N), (ws_scales, N, N), (sx_scales, 2 * N, O)):
+            rows = scales[0].bitcast(I32).rearrange("(a b r) n -> b r a n", a=2, b=2)
+            for b in range(2):
+                nc.sync.dma_start(late_stage[QUAD * b : QUAD * b + PACK, :, first // 4 : (first + width) // 4], rows[b])
         ws_t = load_bytes(ws_words[0], 2 * N, "ws_t")
         sx_t = load_bytes(sx_words[0].rearrange("p c r -> p (c r)"), 4 * O, "sx_t")
         wb_t = load_bytes(wb_words[0], 2 * N, "wb_t")
@@ -89,7 +91,6 @@ def tile_list_leadlevel_codednote_further_pagetwice_kernel(
         nc.vector.memset(w_plane_raw[:].bitcast(I32), 0)
         xo_plane = sb.tile([P, Z], U8, name="xo_plane")
         nc.vector.memset(xo_plane[:].bitcast(I32), 0)
-        nc.vector.memset(late_plane[:].bitcast(I32), 0)
         pages = [[sb.tile([P, E], F32, name=f"page{h}{s}") for s in range(2)] for h in range(2)]
         for h in range(2):
             for s in range(2):
@@ -182,8 +183,8 @@ def tile_list_leadlevel_codednote_further_pagetwice_kernel(
             nc.vector.tensor_copy(a_t[t][:], a_ps[t])
         for t in range(2, PACK):
             nc.vector.tensor_copy(b_t[t][:], b_ps[t])
-        for q in range(4):
-            nc.vector.tensor_copy(late_plane[QUAD * q : QUAD * q + PACK, :].bitcast(I32), late_stage[:, q, :])
+        for a in range(2):
+            nc.vector.tensor_copy(late_plane[2 * QUAD * a : 2 * QUAD * (a + 1), :].bitcast(I32), late_stage[:, a, :])
         p_ps = [psum.tile([P, O], F32, name=f"p_ps{h}", tag=f"b_ps{2 + h}") for h in range(2)]
         for h in range(2):
             nc.tensor.matmul_mx(

from contextlib import ExitStack

import concourse.mybir as mybir

F32 = mybir.dt.float32
BF16 = mybir.dt.bfloat16
I32 = mybir.dt.int32
U32 = mybir.dt.uint32
U16 = mybir.dt.uint16
U8 = mybir.dt.uint8
FP8X4 = mybir.dt.float8_e4m3fn_x4
FP4X4 = mybir.dt.float4_e2m1fn_x4
COPY = mybir.ActivationFunctionType.Copy
ALU = mybir.AluOpType

P = 128
PACK = 4
QUAD = 32
T, J, R, Z, X, O, N, E = 1024, 256, 512, 1024, 512, 128, 256, 512

FLOPS = 335544320


def tile_list_leadlevel_codednote_further_pagetwice_kernel(
    tc, xo_words, xo_scales, cq, gs, w_words, w_scales, w2_words, w2_scales, tb, wb_words, wb_scales,
    sx_words, sx_scales, ws_words, ws_scales, offs, offs2, offs3, offs4, offs5, offs6, offs7, out
):
    nc = tc.nc

    def by_quadrant(scales):
        return scales[0].bitcast(I32).rearrange("(q r) n -> r q n", r=PACK)

    with ExitStack() as ctx:
        lists = ctx.enter_context(tc.tile_pool(name="lists", bufs=1))
        sb = ctx.enter_context(tc.tile_pool(name="sb", bufs=1))
        reused = ctx.enter_context(tc.tile_pool(name="reused", bufs=1))
        psum = ctx.enter_context(tc.psum_pool(name="psum", bufs=1))

        def load_list(src, name):
            tile = lists.tile([P, src.shape[1]], U16, name=name)
            nc.sync.dma_start(tile[:], src)
            return tile

        def load_bytes(src, width, name):
            tile = sb.tile([P, width], U8, name=name, align_bytes=64)
            nc.sync.dma_start(tile[:].bitcast(I32), src.bitcast(I32))
            return tile

        cq_rows = cq.rearrange("(p i) t -> i p t", i=PACK)
        tb_rows = tb.rearrange("(p i) x -> i p x", i=PACK)
        cq_t = [sb.tile([P, T], F32, name=f"cq{i}") for i in range(PACK)]
        tb_t = [sb.tile([P, X], F32, name=f"tb{i}") for i in range(PACK)]

        idx = load_list(offs, "idx")
        nc.sync.dma_start(cq_t[0][:], cq_rows[0])
        idx2 = load_list(offs2, "idx2")
        for i in range(1, PACK):
            nc.sync.dma_start(cq_t[i][:], cq_rows[i])
        w_raw = load_bytes(w_words[0], 2 * R, "w_raw")
        w2_raw = load_bytes(w2_words[0], 2 * R, "w2_raw")
        xo_t = reused.tile([P, Z], I32, name="xo_t", offset=0)
        nc.sync.dma_start(xo_t[:], xo_words[0].rearrange("p c r -> p (c r)").bitcast(I32))
        idx3 = load_list(offs3, "idx3")
        nc.sync.dma_start(tb_t[0][:], tb_rows[0])
        idx4 = load_list(offs4, "idx4")
        idx5 = load_list(offs5, "idx5")
        for i in range(1, PACK):
            nc.sync.dma_start(tb_t[i][:], tb_rows[i])
        late_stage = sb.tile([2 * QUAD, 2, (N + N + O) // 4], I32, name="late_stage")
        nc.vector.memset(late_stage[:], 0)
        for scales, first, width in ((wb_scales, 0, N), (ws_scales, N, N), (sx_scales, 2 * N, O)):
            rows = scales[0].bitcast(I32).rearrange("(a b r) n -> b r a n", a=2, b=2)
            for b in range(2):
                nc.sync.dma_start(late_stage[QUAD * b : QUAD * b + PACK, :, first // 4 : (first + width) // 4], rows[b])
        ws_t = load_bytes(ws_words[0], 2 * N, "ws_t")
        sx_t = load_bytes(sx_words[0].rearrange("p c r -> p (c r)"), 4 * O, "sx_t")
        wb_t = load_bytes(wb_words[0], 2 * N, "wb_t")
        idx6 = load_list(offs6, "idx6")
        idx7 = load_list(offs7, "idx7")

        gs_t = sb.tile([P, PACK], F32, name="gs_t")
        nc.scalar.dma_start(gs_t[:], gs.rearrange("(p i) o -> p (i o)", i=PACK))
        w_stage = sb.tile([PACK, 4, 2 * R // 4], I32, name="w_stage")
        nc.scalar.dma_start(w_stage[:, :, 0 : R // 4], by_quadrant(w_scales))
        nc.scalar.dma_start(w_stage[:, :, R // 4 :], by_quadrant(w2_scales))
        xo_stage = sb.tile([PACK, 4, Z // 4], I32, name="xo_stage")
        nc.scalar.dma_start(xo_stage[:], by_quadrant(xo_scales))

        w_plane_raw = sb.tile([P, 2 * R], U8, name="w_plane_raw")
        late_plane = sb.tile([P, N + N + O], U8, name="late_plane", align_bytes=64)
        nc.vector.memset(w_plane_raw[:].bitcast(I32), 0)
        xo_plane = sb.tile([P, Z], U8, name="xo_plane")
        nc.vector.memset(xo_plane[:].bitcast(I32), 0)
        pages = [[sb.tile([P, E], F32, name=f"page{h}{s}") for s in range(2)] for h in range(2)]
        for h in range(2):
            for s in range(2):
                nc.vector.memset(pages[h][s][:], 0.0)

        for q in range(4):
            nc.vector.tensor_copy(w_plane_raw[QUAD * q : QUAD * q + PACK, :].bitcast(I32), w_stage[:, q, :])
            nc.vector.tensor_copy(xo_plane[QUAD * q : QUAD * q + PACK, :].bitcast(I32), xo_stage[:, q, :])
        w_plane = sb.tile([P, 2 * R], U8, name="w_plane", align_bytes=64)
        nc.vector.tensor_copy(
            w_plane[:].rearrange("p (u t m) -> p u t m", u=2, t=PACK),
            w_plane_raw[:].rearrange("p (u m t) -> p u t m", u=2, t=PACK),
        )
        note_scales = sb.tile([P, J], U8, name="note_scales", align_bytes=64)
        nc.vector.tensor_copy(note_scales[:], xo_plane[:].indirect(idx2[:]))


        x1 = sb.tile([P, PACK, J], BF16, name="x1")
        x1_il = sb.tile([P, J, PACK], BF16, name="x1_il", align_bytes=64)
        for i in range(PACK):
            nc.scalar.activation(x1[:, i, :], cq_t[i][:].indirect(idx[:]), COPY, scale=gs_t[:, i : i + 1])
            if i == 1:
                nc.vector.tensor_copy(x1_il[:, :, 0:2], x1[:, 0:2, :].rearrange("p t j -> p j t"))
        halves = (slice(0, J // 2), slice(J // 2, J))
        for half in halves:
            nc.vector.tensor_copy(x1_il[:, half, 2:4], x1[:, 2:4, half].rearrange("p t j -> p j t"))
        x1_codes = sb.tile([P, J], U32, name="x1_codes", align_bytes=64)
        x1_scales = sb.tile([P, J], U8, name="x1_scales", align_bytes=64)

        w_t = sb.tile([P, 2 * R], U8, name="w_t", align_bytes=64)
        w2_t = sb.tile([P, 2 * R], U8, name="w2_t", align_bytes=64)
        nc.scalar.copy(
            w_t[:].bitcast(U16).rearrange("p (t m) -> p t m", t=PACK),
            w_raw[:].bitcast(U16).rearrange("p (m t) -> p t m", t=PACK),
        )
        nc.scalar.copy(
            w2_t[:].bitcast(U16).rearrange("p (t m) -> p t m", t=PACK),
            w2_raw[:].bitcast(U16).rearrange("p (m t) -> p t m", t=PACK),
        )
        for half in halves:
            nc.vector.quantize_mx(
                out=x1_codes[:, half].bitcast(FP8X4),
                scales=x1_scales[:, half],
                in_=x1_il[:, half, :].rearrange("p j t -> p (j t)"),
            )
        note_words = sb.tile([P, J], U32, name="note_words", align_bytes=64)
        nc.vector.tensor_copy(note_words[:], xo_t[:].bitcast(U32).indirect(idx2[:]))

        a_ps = [psum.tile([P, J], F32, name=f"a_ps{t}")[:] for t in range(PACK)]
        b_ps = [psum.tile([P, J], F32, name=f"b_ps{t}")[:] for t in range(PACK)]
        a_t = [sb.tile([P, J], F32, name="a0")]
        a_t.extend(reused.tile([P, J], F32, name=f"a{t}", offset=4 * J * t) for t in range(1, PACK))

        def first_product(t, cols):
            nc.tensor.matmul_mx(
                out=a_ps[t][:, cols],
                lhsT=w_t[:, 2 * P * t : 2 * P * (t + 1)].bitcast(FP4X4),
                lhsT_scale=w_plane[:, P * t : P * (t + 1)],
                rhs=x1_codes[:, cols].bitcast(FP8X4),
                rhs_scale=x1_scales[:, cols],
                start=True,
                stop=True,
            )

        first_product(0, halves[0])
        nc.scalar.copy(a_t[0][:, halves[0]], a_ps[0][:, halves[0]])
        for t in range(1, PACK):
            first_product(t, slice(0, J))
        first_product(0, halves[1])
        for t in range(PACK):
            nc.tensor.matmul_mx(
                out=b_ps[t],
                lhsT=w2_t[:, 2 * P * t : 2 * P * (t + 1)].bitcast(FP4X4),
                lhsT_scale=w_plane[:, R + P * t : R + P * (t + 1)],
                rhs=note_words[:].bitcast(FP8X4),
                rhs_scale=note_scales[:],
                start=True,
                stop=True,
            )

        b_t = [sb.tile([P, J], F32, name=f"b{t}") for t in range(PACK)]
        level = sb.tile([P, PACK, O], F32, name="level")
        lead = sb.tile([P, PACK, O], F32, name="lead")
        hid = sb.tile([P, O, PACK], BF16, name="hid", align_bytes=64)
        nc.vector.tensor_copy(a_t[1][:], a_ps[1])
        nc.scalar.copy(a_t[0][:, halves[1]], a_ps[0][:, halves[1]])
        for t in range(2):
            nc.vector.tensor_copy(b_t[t][:], b_ps[t])
        for t in range(2, PACK):
            nc.vector.tensor_copy(a_t[t][:], a_ps[t])
        for t in range(2, PACK):
            nc.vector.tensor_copy(b_t[t][:], b_ps[t])
        for a in range(2):
            nc.vector.tensor_copy(late_plane[2 * QUAD * a : 2 * QUAD * (a + 1), :].bitcast(I32), late_stage[:, a, :])
        p_ps = [psum.tile([P, O], F32, name=f"p_ps{h}", tag=f"b_ps{2 + h}") for h in range(2)]
        for h in range(2):
            nc.tensor.matmul_mx(
                out=p_ps[h][:],
                lhsT=ws_t[:, 2 * P * h : 2 * P * (h + 1)].bitcast(FP4X4),
                lhsT_scale=late_plane[:, N + P * h : N + P * (h + 1)],
                rhs=sx_t[:].bitcast(FP8X4),
                rhs_scale=late_plane[:, 2 * N :],
                start=True,
                stop=False,
            )

        for pair in (slice(0, 2), slice(2, 4)):
            for t in range(pair.start, pair.stop):
                nc.scalar.activation(level[:, t, :], tb_t[t][:].indirect(idx3[:]), COPY, scale=a_t[t][:, 0:1])
            for t in range(pair.start, pair.stop):
                nc.scalar.activation(lead[:, t, :], a_t[t][:].indirect(idx4[:]), COPY, scale=b_t[t][:, 0:1])
            minus = sb.tile([P, 2, O], F32, name=f"minus{pair.start}", tag=f"tb{pair.stop - 1}")
            for t in range(pair.start, pair.stop):
                nc.scalar.activation(minus[:, t % 2, :], b_t[t][:].indirect(idx5[:]), COPY, scale=a_t[t][:, P : P + 1])
            larger = sb.tile([P, 2, O], F32, name=f"larger{pair.start}", tag="late_stage" if pair.start else "larger")
            nc.vector.tensor_tensor(larger[:], level[:, pair, :], lead[:, pair, :], ALU.max)
            nc.vector.tensor_tensor(
                hid[:, :, pair],
                larger[:].rearrange("p t o -> p o t"),
                minus[:].rearrange("p t o -> p o t"),
                ALU.subtract,
            )

        hid_codes = sb.tile([P, O], U32, name="hid_codes", align_bytes=64)
        hid_scales = sb.tile([P, O], U8, name="hid_scales", align_bytes=64)
        nc.vector.quantize_mx(
            out=hid_codes[:].bitcast(FP8X4), scales=hid_scales[:], in_=hid[:].rearrange("p o t -> p (o t)")
        )
        for h in range(2):
            nc.tensor.matmul_mx(
                out=p_ps[h][:],
                lhsT=wb_t[:, 2 * P * h : 2 * P * (h + 1)].bitcast(FP4X4),
                lhsT_scale=late_plane[:, P * h : P * (h + 1)],
                rhs=hid_codes[:].bitcast(FP8X4),
                rhs_scale=hid_scales[:],
                start=False,
                stop=True,
            )

        p_t = [sb.tile([P, O], F32, name=f"p{h}") for h in range(2)]
        nc.vector.tensor_copy(p_t[0][:], p_ps[0][:])
        nc.scalar.copy(p_t[1][:], p_ps[1][:])
        nc.vector.tensor_copy(pages[0][0][:].indirect(idx6[:]), p_t[0][:])
        nc.scalar.activation(pages[0][1][:].indirect(idx7[:]), p_t[0][:], COPY)
        nc.vector.tensor_copy(pages[1][1][:].indirect(idx7[:]), p_t[1][:])
        nc.scalar.activation(pages[1][0][:].indirect(idx6[:]), p_t[1][:], COPY)
        for h in range(2):
            for c in range(2):
                cols = slice(c * E // 2, (c + 1) * E // 2)
                y = sb.tile([P, E // 2], F32, name=f"y{h}{c}")
                nc.vector.tensor_tensor(y[:], pages[h][0][:, cols], pages[h][1][:, cols], ALU.add)
                nc.sync.dma_start(out[P * h : P * (h + 1), cols], y[:])
